import numpy as np
import ml_dtypes


def mxq(x, axis, fmt="e4m3"):
    dtype, down = {"e4m3": (ml_dtypes.float8_e4m3fn, 7), "e5m2": (ml_dtypes.float8_e5m2, 14)}[fmt]
    v = np.moveaxis(np.asarray(x, np.float32).astype(ml_dtypes.bfloat16).astype(np.float64), axis, -1)
    blocks = v.reshape(v.shape[:-1] + (-1, 32))
    amax = np.abs(blocks).max(-1, keepdims=True)
    byte = np.maximum(np.where(amax > 0, np.frexp(amax)[1] - 1 + 127, 0) - down, 1)
    scale = np.exp2(byte - 127.0)
    codes = (blocks / scale).astype(np.float32).astype(dtype).astype(np.float64)
    return np.moveaxis((codes * scale).reshape(v.shape), -1, axis)


WIDE = False


def mx_kscale(k):
    if not WIDE:
        return np.ones(k)
    levels = np.array([30, -30])
    if k % 512:
        return np.exp2(np.random.permutation(np.resize(levels, k // 32))).repeat(32)
    a = np.empty((k // 512, 16))
    for p in range(k // 512):
        a[p, :8] = np.random.permutation(np.resize(levels, 8))
        for g in range(8):
            far = levels[np.abs(levels - a[p, g]) >= 10]
            a[p, g + 8] = far[np.random.randint(len(far))]
    return np.exp2(a.ravel()).repeat(32)


def f64(x):
    return np.asarray(x).astype(np.float64)


def striped(idx):
    return np.tile(np.asarray(idx).reshape(-1, 16).T, (8, 1)).astype(np.uint16)


def unstriped(offs):
    return offs[:16].T.reshape(-1).astype(np.int64)


E2M1 = np.array([0.0, 0.5, 1.0, 1.5, 2.0, 3.0, 4.0, 6.0, -0.0, -0.5, -1.0, -1.5, -2.0, -3.0, -4.0, -6.0])


def pack_weight(w, fmt):
    k, n = w.shape
    w = f64(np.asarray(w, np.float32).astype(ml_dtypes.bfloat16)).reshape(k // 32, 32, n)
    amax = np.abs(w).max(1)
    if fmt in ("e4m3", "e5m2"):
        byte = np.frexp(amax)[1] - 1 + 127 - (7 if fmt == "e4m3" else 14)
    else:
        mant, ex = np.frexp(amax / 6.0)
        byte = np.where(mant > 0.5, ex, ex - 1) + 127
    byte = np.clip(np.where(amax > 0, byte, 1), 1, 254)
    scaled = (w * np.exp2(127.0 - byte)[:, None, :]).reshape(k, n).astype(np.float32)
    by_word = np.ascontiguousarray(scaled.reshape(k // 512, 128, 4, n).transpose(0, 1, 3, 2))
    if fmt in ("e4m3", "e5m2"):
        words = by_word.astype(ml_dtypes.float8_e4m3fn if fmt == "e4m3" else ml_dtypes.float8_e5m2).view(np.uint8)
    else:
        c = by_word.astype(ml_dtypes.float4_e2m1fn).view(np.uint8) & 0xF
        words = (c[..., 0::2] | (c[..., 1::2] << 4)).reshape(k // 512, 128, 2 * n)
    return np.ascontiguousarray(words), np.ascontiguousarray(byte.astype(np.uint8).reshape(k // 512, 16, n))


def unpack_weight(words, scales, fmt):
    g, _, n = scales.shape
    words = np.ascontiguousarray(words).reshape(g, 128, n, -1)
    if fmt in ("e4m3", "e5m2"):
        vals = words.view(ml_dtypes.float8_e4m3fn if fmt == "e4m3" else ml_dtypes.float8_e5m2).astype(np.float64)
    else:
        nib = np.empty((g, 128, n, 4), np.uint8)
        nib[..., 0::2] = words & 0xF
        nib[..., 1::2] = words >> 4
        vals = E2M1[nib]
    vals = vals * np.repeat(np.exp2(scales.astype(np.float64) - 127.0), 8, axis=1)[..., None]
    return vals.transpose(0, 1, 3, 2).reshape(g * 512, n)


K, T, J, I, V = 1024, 1024, 256, 256, 1024


def setup_inputs():
    n = np.random.standard_normal
    idx = np.random.permutation(T)[:J]
    idx2 = np.random.permutation(T)[:J]
    idx3 = np.random.permutation(V)[:I]
    fk = mx_kscale(K)
    kyp = pack_weight(n((K, V)) / fk[:, None], "e5m2")
    return {
        "xf": (n((K, T)) * 0.03).astype(np.float32),
        "fk": (np.random.uniform(0.5, 2.0, (K, 1)) * fk[:, None]).astype(np.float32),
        "ky_words": kyp[0],
        "ky_scales": kyp[1],
        "bi": (np.random.uniform(-0.7, 0.7, (1, I))).astype(np.float32),
        "offs": striped(idx),
        "offs2": striped(idx2),
        "offs3": striped(idx3),
    }


def reference(xf, fk, ky_words, ky_scales, bi, offs, offs2, offs3):
    idx = unstriped(offs)
    idx2 = unstriped(offs2)
    idx3 = unstriped(offs3)
    kyu = unpack_weight(ky_words, ky_scales, "e5m2")
    u = (f64(xf)[:, idx] - f64(xf)[:, idx2]) * f64(fk)
    uq = mxq(u, 0, "e5m2")
    kyidx3g = kyu[:, idx3]
    a0 = uq.T @ kyidx3g
    a = a0 + f64(bi)
    a1 = np.pad(a, ((0, 0), (1, 0)))[:, :I]
    y = np.abs(a - a1)
    return y

@@ -1,0 +1,160 @@
+from contextlib import ExitStack
+
+import concourse.mybir as mybir
+from concourse.masks import make_identity
+
+K, T, J, I, V = 1024, 1024, 256, 256, 1024
+FLOPS = 2 * K * J * I
+
+F32 = mybir.dt.float32
+BF16 = mybir.dt.bfloat16
+I32 = mybir.dt.int32
+U32 = mybir.dt.uint32
+U16 = mybir.dt.uint16
+U8 = mybir.dt.uint8
+E5X4 = mybir.dt.float8_e5m2_x4
+ALU = mybir.AluOpType
+ACT = mybir.ActivationFunctionType
+
+P = 128
+PACK = 4
+PASSES = K // (P * PACK)
+PLANES = PASSES * PACK
+PAD = 4
+VECTOR_GATHERS = (0, 1, 2, 3, 7,)
+GROUPS = ((0, 2), (2, 4), (4, 6), (6, 8))
+
+
+def tile_list_scores_gaps_listed_steps_kernel(tc, xf, fk, ky_words, ky_scales, bi, offs, offs2, offs3, out):
+    nc = tc.nc
+    with ExitStack() as ctx:
+        keep = ctx.enter_context(tc.tile_pool(name="keep", bufs=1))
+        psum = ctx.enter_context(tc.psum_pool(name="psum", bufs=1))
+
+        list1 = keep.tile([P, J // 16], U16, name="list1")
+        list2 = keep.tile([P, J // 16], U16, name="list2")
+        list3 = keep.tile([P, I // 16], U16, name="list3")
+        planes = [keep.tile([P, T], F32, name="plane%d" % q) for q in range(PLANES)]
+        words = [keep.tile([P, V], I32, name="words%d" % z) for z in range(PASSES)]
+        scales = keep.tile([P, PASSES, V], U8, name="scales")
+        factor = keep.tile([P, PASSES, 2 * PACK], F32, name="factor")
+        bias_col = keep.tile([P, 2], F32, name="bias_col")
+        ident = keep.tile([P, P], F32, name="ident")
+        bias = keep.tile([P, I], F32, name="bias")
+        scores = [keep.tile([P, PAD + I], F32, name="scores%d" % m) for m in range(J // P)]
+
+        nc.vector.memset(scales[:].rearrange("p z c -> p (z c)").bitcast(I32), 0)
+        make_identity(nc, ident[:])
+        for m in range(J // P):
+            nc.vector.memset(scores[m][:, PAD - 1 : PAD], 0.0)
+
+        x_rows = xf.rearrange("(z p t) c -> z t p c", p=P, t=PACK)
+
+        def load_plane(q):
+            nc.sync.dma_start(out=planes[q][:], in_=x_rows[q // PACK, q % PACK])
+
+        def load_scales(quad):
+            nc.sync.dma_start(
+                out=scales[32 * quad : 32 * quad + 4].bitcast(I32),
+                in_=ky_scales[:, 4 * quad : 4 * quad + 4, :].rearrange("z r c -> r z c").bitcast(I32),
+            )
+
+        load_plane(0)
+        nc.sync.dma_start(list2[:], offs2)
+        nc.sync.dma_start(list1[:], offs)
+        load_plane(1)
+        nc.sync.dma_start(out=factor[:, :, 0:PACK], in_=fk.rearrange("(z p t) o -> p z (t o)", p=P, t=PACK))
+        load_plane(2)
+        nc.sync.dma_start(list3[:], offs3)
+        load_scales(0)
+        load_scales(1)
+        load_plane(3)
+        load_scales(2)
+        load_scales(3)
+        for q in range(4, PLANES):
+            load_plane(q)
+        nc.sync.dma_start(out=bias_col[:], in_=bi.rearrange("o (p m) -> p (o m)", m=2))
+        for z in range(PASSES):
+            nc.sync.dma_start(out=words[z][:], in_=ky_words[z].rearrange("p n t -> p (n t)").bitcast(I32))
+
+        woven = [keep.tile([P, J, PACK], BF16, name="woven%d" % z, align_bytes=64) for z in range(PASSES)]
+        u_codes = [keep.tile([P, J], U32, name="u_codes%d" % z, align_bytes=64) for z in range(PASSES)]
+        u_scales = [keep.tile([P, J], U8, name="u_scales%d" % z, align_bytes=64) for z in range(PASSES)]
+        k_codes = [keep.tile([P, I], U32, name="k_codes%d" % z, align_bytes=64) for z in range(PASSES)]
+        k_scales = [keep.tile([P, I], U8, name="k_scales%d" % z, align_bytes=64) for z in range(PASSES)]
+        acc = [psum.tile([P, I], F32, name="acc%d" % m) for m in range(J // P)]
+        bias_ps = psum.tile([P, 2, P], F32, name="bias_ps")
+        gaps = [keep.tile([P, PACK, J], F32, name="gaps%d" % z) for z in range(PASSES)]
+
+        def gap_planes(q0, q1):
+            first = keep.tile([P, q1 - q0, J], F32, name="first%d" % q0)
+            second = keep.tile([P, q1 - q0, J], F32, name="second%d" % q0)
+            for q in range(q0, q1):
+                nc.scalar.activation(second[:, q - q0, :], planes[q][:].indirect(list2[:]), ACT.Copy)
+                if q in VECTOR_GATHERS:
+                    nc.vector.tensor_copy(first[:, q - q0, :], planes[q][:].indirect(list1[:]))
+                else:
+                    nc.scalar.activation(first[:, q - q0, :], planes[q][:].indirect(list1[:]), ACT.Copy)
+            z, t0 = divmod(q0, PACK)
+            nc.vector.tensor_tensor(gaps[z][:, t0 : t0 + q1 - q0, :], first[:], second[:], ALU.subtract)
+
+        def weave(z):
+            nc.vector.tensor_tensor(
+                woven[z][:].rearrange("p (c i) t -> p c t i", i=4),
+                gaps[z][:].rearrange("p t (c i) -> p c t i", i=4),
+                factor[:, z, 0:PACK].unsqueeze(1).unsqueeze(3).broadcast_to([P, J // 4, PACK, 4]),
+                ALU.mult,
+            )
+
+        def quantise(z):
+            nc.vector.quantize_mx(
+                out=u_codes[z][:].bitcast(E5X4),
+                scales=u_scales[z][:],
+                in_=woven[z][:].rearrange("p j t -> p (j t)"),
+            )
+
+        def gather_words(z):
+            nc.vector.tensor_copy(k_codes[z][:], words[z][:].bitcast(U32).indirect(list3[:]))
+
+        def gather_scales(z):
+            nc.vector.tensor_copy(k_scales[z][:], scales[:, z, :].indirect(list3[:]))
+
+        def multiply(z):
+            for m in range(J // P):
+                rows = slice(m * P, (m + 1) * P)
+                nc.tensor.matmul_mx(
+                    out=acc[m][:],
+                    lhsT=u_codes[z][:, rows].bitcast(E5X4),
+                    lhsT_scale=u_scales[z][:, rows],
+                    rhs=k_codes[z][:].bitcast(E5X4),
+                    rhs_scale=k_scales[z][:],
+                    start=(z == 0),
+                    stop=(z == PASSES - 1),
+                )
+
+        for m in range(2):
+            nc.tensor.transpose(bias_ps[:, m, :], bias_col[:, m : m + 1].to_broadcast([P, P]), ident[:])
+
+        for q0, q1 in GROUPS:
+            gap_planes(q0, q1)
+            if q1 == PACK:
+                weave(0)
+                gather_scales(0)
+                quantise(0)
+                gather_scales(1)
+        gather_words(0)
+        weave(1)
+        multiply(0)
+        gather_words(1)
+        quantise(1)
+        multiply(1)
+        nc.scalar.copy(bias[:].rearrange("p (r m) -> p r m", m=2), bias_ps[:].rearrange("p m r -> p r m"))
+
+        steps = [keep.tile([P, I], F32, name="steps%d" % m) for m in range(J // P)]
+        result = [keep.tile([P, I], F32, name="result%d" % m) for m in range(J // P)]
+        for m in range(J // P):
+            nc.vector.tensor_tensor(scores[m][:, PAD:], acc[m][:], bias[:], ALU.add)
+        for m in range(J // P):
+            nc.vector.tensor_tensor(steps[m][:], scores[m][:, PAD:], scores[m][:, PAD - 1 : PAD - 1 + I], ALU.subtract)
+            nc.scalar.activation(result[m][:], steps[m][:], ACT.Abs)
+            nc.sync.dma_start(out=out[m * P : (m + 1) * P, :], in_=result[m][:])

@@ -21,7 +21,7 @@ PACK = 4
 PASSES = K // (P * PACK)
 PLANES = PASSES * PACK
 PAD = 4
-VECTOR_GATHERS = (0, 1, 2, 3, 7,)
+VECTOR_GATHERS = (0, 1, 7,)
 GROUPS = ((0, 2), (2, 4), (4, 6), (6, 8))
 
 
@@ -37,16 +37,18 @@ def tile_list_scores_gaps_listed_steps_kernel(tc, xf, fk, ky_words, ky_scales, b
         planes = [keep.tile([P, T], F32, name="plane%d" % q) for q in range(PLANES)]
         words = [keep.tile([P, V], I32, name="words%d" % z) for z in range(PASSES)]
         scales = keep.tile([P, PASSES, V], U8, name="scales")
-        factor = keep.tile([P, PASSES, 2 * PACK], F32, name="factor")
+        factor = [keep.tile([P, PACK], F32, name="factor%d" % z) for z in range(PASSES)]
         bias_col = keep.tile([P, 2], F32, name="bias_col")
         ident = keep.tile([P, P], F32, name="ident")
         bias = keep.tile([P, I], F32, name="bias")
         scores = [keep.tile([P, PAD + I], F32, name="scores%d" % m) for m in range(J // P)]
 
-        nc.vector.memset(scales[:].rearrange("p z c -> p (z c)").bitcast(I32), 0)
+        zero = keep.tile([P, 1], F32, name="zero")
+        nc.vector.memset(zero[:], 0.0)
+        nc.gpsimd.memset(scales[:].rearrange("p z c -> p (z c)").bitcast(I32), 0)
         make_identity(nc, ident[:])
         for m in range(J // P):
-            nc.vector.memset(scores[m][:, PAD - 1 : PAD], 0.0)
+            nc.scalar.activation(scores[m][:, PAD - 1 : PAD], zero[:], ACT.Copy)
 
         x_rows = xf.rearrange("(z p t) c -> z t p c", p=P, t=PACK)
 
@@ -59,23 +61,28 @@ def tile_list_scores_gaps_listed_steps_kernel(tc, xf, fk, ky_words, ky_scales, b
                 in_=ky_scales[:, 4 * quad : 4 * quad + 4, :].rearrange("z r c -> r z c").bitcast(I32),
             )
 
+        def load_words(z):
+            nc.sync.dma_start(out=words[z][:], in_=ky_words[z].rearrange("p n t -> p (n t)").bitcast(I32))
+
+        def load_factor(z):
+            nc.sync.dma_start(out=factor[z][:], in_=fk.rearrange("(z p t) o -> z p (t o)", p=P, t=PACK)[z])
+
         load_plane(0)
         nc.sync.dma_start(list2[:], offs2)
         nc.sync.dma_start(list1[:], offs)
         load_plane(1)
-        nc.sync.dma_start(out=factor[:, :, 0:PACK], in_=fk.rearrange("(z p t) o -> p z (t o)", p=P, t=PACK))
-        load_plane(2)
         nc.sync.dma_start(list3[:], offs3)
-        load_scales(0)
-        load_scales(1)
+        load_plane(2)
+        for quad in range(4):
+            load_scales(quad)
         load_plane(3)
-        load_scales(2)
-        load_scales(3)
+        load_factor(0)
         for q in range(4, PLANES):
             load_plane(q)
+        load_words(0)
+        load_factor(1)
+        load_words(1)
         nc.sync.dma_start(out=bias_col[:], in_=bi.rearrange("o (p m) -> p (o m)", m=2))
-        for z in range(PASSES):
-            nc.sync.dma_start(out=words[z][:], in_=ky_words[z].rearrange("p n t -> p (n t)").bitcast(I32))
 
         woven = [keep.tile([P, J, PACK], BF16, name="woven%d" % z, align_bytes=64) for z in range(PASSES)]
         u_codes = [keep.tile([P, J], U32, name="u_codes%d" % z, align_bytes=64) for z in range(PASSES)]
@@ -102,15 +109,15 @@ def tile_list_scores_gaps_listed_steps_kernel(tc, xf, fk, ky_words, ky_scales, b
             nc.vector.tensor_tensor(
                 woven[z][:].rearrange("p (c i) t -> p c t i", i=4),
                 gaps[z][:].rearrange("p t (c i) -> p c t i", i=4),
-                factor[:, z, 0:PACK].unsqueeze(1).unsqueeze(3).broadcast_to([P, J // 4, PACK, 4]),
+                factor[z][:].unsqueeze(1).unsqueeze(3).broadcast_to([P, J // 4, PACK, 4]),
                 ALU.mult,
             )
 
-        def quantise(z):
+        def quantise(z, j0, j1):
             nc.vector.quantize_mx(
-                out=u_codes[z][:].bitcast(E5X4),
-                scales=u_scales[z][:],
-                in_=woven[z][:].rearrange("p j t -> p (j t)"),
+                out=u_codes[z][:, j0:j1].bitcast(E5X4),
+                scales=u_scales[z][:, j0:j1],
+                in_=woven[z][:, j0:j1, :].rearrange("p j t -> p (j t)"),
             )
 
         def gather_words(z):
@@ -137,16 +144,18 @@ def tile_list_scores_gaps_listed_steps_kernel(tc, xf, fk, ky_words, ky_scales, b
 
         for q0, q1 in GROUPS:
             gap_planes(q0, q1)
+            if q1 == 2:
+                gather_scales(0)
+                gather_scales(1)
             if q1 == PACK:
                 weave(0)
-                gather_scales(0)
-                quantise(0)
-                gather_scales(1)
+                quantise(0, 0, J)
         gather_words(0)
         weave(1)
         multiply(0)
         gather_words(1)
-        quantise(1)
+        for m in range(J // P):
+            quantise(1, m * P, (m + 1) * P)
         multiply(1)
         nc.scalar.copy(bias[:].rearrange("p (r m) -> p r m", m=2), bias_ps[:].rearrange("p m r -> p r m"))
 
@@ -157,4 +166,4 @@ def tile_list_scores_gaps_listed_steps_kernel(tc, xf, fk, ky_words, ky_scales, b
         for m in range(J // P):
             nc.vector.tensor_tensor(steps[m][:], scores[m][:, PAD:], scores[m][:, PAD - 1 : PAD - 1 + I], ALU.subtract)
             nc.scalar.activation(result[m][:], steps[m][:], ACT.Abs)
-            nc.sync.dma_start(out=out[m * P : (m + 1) * P, :], in_=result[m][:])
+            (nc.sync if m == 0 else nc.scalar).dma_start(out=out[m * P : (m + 1) * P, :], in_=result[m][:])

@@ -21,7 +21,7 @@ PACK = 4
 PASSES = K // (P * PACK)
 PLANES = PASSES * PACK
 PAD = 4
-VECTOR_GATHERS = (0, 1, 7,)
+VECTOR_GATHERS = (0, 1, 3, 5, 7,)
 GROUPS = ((0, 2), (2, 4), (4, 6), (6, 8))
 
 
@@ -79,10 +79,10 @@ def tile_list_scores_gaps_listed_steps_kernel(tc, xf, fk, ky_words, ky_scales, b
         load_factor(0)
         for q in range(4, PLANES):
             load_plane(q)
+        nc.sync.dma_start(out=bias_col[:], in_=bi.rearrange("o (p m) -> p (o m)", m=2))
         load_words(0)
         load_factor(1)
         load_words(1)
-        nc.sync.dma_start(out=bias_col[:], in_=bi.rearrange("o (p m) -> p (o m)", m=2))
 
         woven = [keep.tile([P, J, PACK], BF16, name="woven%d" % z, align_bytes=64) for z in range(PASSES)]
         u_codes = [keep.tile([P, J], U32, name="u_codes%d" % z, align_bytes=64) for z in range(PASSES)]

@@ -21,7 +21,7 @@ PACK = 4
 PASSES = K // (P * PACK)
 PLANES = PASSES * PACK
 PAD = 4
-VECTOR_GATHERS = (0, 1, 3, 5, 7,)
+VECTOR_GATHERS = (0, 1, 2, 3, 7,)
 GROUPS = ((0, 2), (2, 4), (4, 6), (6, 8))
 
 
@@ -45,7 +45,7 @@ def tile_list_scores_gaps_listed_steps_kernel(tc, xf, fk, ky_words, ky_scales, b
 
         zero = keep.tile([P, 1], F32, name="zero")
         nc.vector.memset(zero[:], 0.0)
-        nc.gpsimd.memset(scales[:].rearrange("p z c -> p (z c)").bitcast(I32), 0)
+        nc.vector.memset(scales[:].rearrange("p z c -> p (z c)").bitcast(I32), 0)
         make_identity(nc, ident[:])
         for m in range(J // P):
             nc.scalar.activation(scores[m][:, PAD - 1 : PAD], zero[:], ACT.Copy)
@@ -71,13 +71,14 @@ def tile_list_scores_gaps_listed_steps_kernel(tc, xf, fk, ky_words, ky_scales, b
         nc.sync.dma_start(list2[:], offs2)
         nc.sync.dma_start(list1[:], offs)
         load_plane(1)
-        nc.sync.dma_start(list3[:], offs3)
+        load_factor(0)
         load_plane(2)
         for quad in range(4):
             load_scales(quad)
         load_plane(3)
-        load_factor(0)
-        for q in range(4, PLANES):
+        load_plane(4)
+        nc.sync.dma_start(list3[:], offs3)
+        for q in range(5, PLANES):
             load_plane(q)
         nc.sync.dma_start(out=bias_col[:], in_=bi.rearrange("o (p m) -> p (o m)", m=2))
         load_words(0)
@@ -144,12 +145,11 @@ def tile_list_scores_gaps_listed_steps_kernel(tc, xf, fk, ky_words, ky_scales, b
 
         for q0, q1 in GROUPS:
             gap_planes(q0, q1)
-            if q1 == 2:
-                gather_scales(0)
-                gather_scales(1)
             if q1 == PACK:
                 weave(0)
+                gather_scales(0)
                 quantise(0, 0, J)
+                gather_scales(1)
         gather_words(0)
         weave(1)
         multiply(0)

from contextlib import ExitStack

import concourse.mybir as mybir
from concourse.masks import make_identity

K, T, J, I, V = 1024, 1024, 256, 256, 1024
FLOPS = 2 * K * J * I

F32 = mybir.dt.float32
BF16 = mybir.dt.bfloat16
I32 = mybir.dt.int32
U32 = mybir.dt.uint32
U16 = mybir.dt.uint16
U8 = mybir.dt.uint8
E5X4 = mybir.dt.float8_e5m2_x4
ALU = mybir.AluOpType
ACT = mybir.ActivationFunctionType

P = 128
PACK = 4
PASSES = K // (P * PACK)
PLANES = PASSES * PACK
PAD = 4
VECTOR_GATHERS = (0, 1, 2, 3, 7,)
GROUPS = ((0, 2), (2, 4), (4, 6), (6, 8))


def tile_list_scores_gaps_listed_steps_kernel(tc, xf, fk, ky_words, ky_scales, bi, offs, offs2, offs3, out):
    nc = tc.nc
    with ExitStack() as ctx:
        keep = ctx.enter_context(tc.tile_pool(name="keep", bufs=1))
        psum = ctx.enter_context(tc.psum_pool(name="psum", bufs=1))

        list1 = keep.tile([P, J // 16], U16, name="list1")
        list2 = keep.tile([P, J // 16], U16, name="list2")
        list3 = keep.tile([P, I // 16], U16, name="list3")
        planes = [keep.tile([P, T], F32, name="plane%d" % q) for q in range(PLANES)]
        words = [keep.tile([P, V], I32, name="words%d" % z) for z in range(PASSES)]
        scales = keep.tile([P, PASSES, V], U8, name="scales")
        factor = [keep.tile([P, PACK], F32, name="factor%d" % z) for z in range(PASSES)]
        bias_col = keep.tile([P, 2], F32, name="bias_col")
        ident = keep.tile([P, P], F32, name="ident")
        bias = keep.tile([P, I], F32, name="bias")
        scores = [keep.tile([P, PAD + I], F32, name="scores%d" % m) for m in range(J // P)]

        zero = keep.tile([P, 1], F32, name="zero")
        nc.vector.memset(zero[:], 0.0)
        nc.vector.memset(scales[:].rearrange("p z c -> p (z c)").bitcast(I32), 0)
        make_identity(nc, ident[:])
        for m in range(J // P):
            nc.scalar.activation(scores[m][:, PAD - 1 : PAD], zero[:], ACT.Copy)

        x_rows = xf.rearrange("(z p t) c -> z t p c", p=P, t=PACK)

        def load_plane(q):
            nc.sync.dma_start(out=planes[q][:], in_=x_rows[q // PACK, q % PACK])

        def load_scales(quad):
            nc.sync.dma_start(
                out=scales[32 * quad : 32 * quad + 4].bitcast(I32),
                in_=ky_scales[:, 4 * quad : 4 * quad + 4, :].rearrange("z r c -> r z c").bitcast(I32),
            )

        def load_words(z):
            nc.sync.dma_start(out=words[z][:], in_=ky_words[z].rearrange("p n t -> p (n t)").bitcast(I32))

        def load_factor(z):
            nc.sync.dma_start(out=factor[z][:], in_=fk.rearrange("(z p t) o -> z p (t o)", p=P, t=PACK)[z])

        load_plane(0)
        nc.sync.dma_start(list2[:], offs2)
        nc.sync.dma_start(list1[:], offs)
        load_plane(1)
        load_factor(0)
        load_plane(2)
        for quad in range(4):
            load_scales(quad)
        load_plane(3)
        load_plane(4)
        nc.sync.dma_start(list3[:], offs3)
        for q in range(5, PLANES):
            load_plane(q)
        nc.sync.dma_start(out=bias_col[:], in_=bi.rearrange("o (p m) -> p (o m)", m=2))
        load_words(0)
        load_factor(1)
        load_words(1)

        woven = [keep.tile([P, J, PACK], BF16, name="woven%d" % z, align_bytes=64) for z in range(PASSES)]
        u_codes = [keep.tile([P, J], U32, name="u_codes%d" % z, align_bytes=64) for z in range(PASSES)]
        u_scales = [keep.tile([P, J], U8, name="u_scales%d" % z, align_bytes=64) for z in range(PASSES)]
        k_codes = [keep.tile([P, I], U32, name="k_codes%d" % z, align_bytes=64) for z in range(PASSES)]
        k_scales = [keep.tile([P, I], U8, name="k_scales%d" % z, align_bytes=64) for z in range(PASSES)]
        acc = [psum.tile([P, I], F32, name="acc%d" % m) for m in range(J // P)]
        bias_ps = psum.tile([P, 2, P], F32, name="bias_ps")
        gaps = [keep.tile([P, PACK, J], F32, name="gaps%d" % z) for z in range(PASSES)]

        def gap_planes(q0, q1):
            first = keep.tile([P, q1 - q0, J], F32, name="first%d" % q0)
            second = keep.tile([P, q1 - q0, J], F32, name="second%d" % q0)
            for q in range(q0, q1):
                nc.scalar.activation(second[:, q - q0, :], planes[q][:].indirect(list2[:]), ACT.Copy)
                if q in VECTOR_GATHERS:
                    nc.vector.tensor_copy(first[:, q - q0, :], planes[q][:].indirect(list1[:]))
                else:
                    nc.scalar.activation(first[:, q - q0, :], planes[q][:].indirect(list1[:]), ACT.Copy)
            z, t0 = divmod(q0, PACK)
            nc.vector.tensor_tensor(gaps[z][:, t0 : t0 + q1 - q0, :], first[:], second[:], ALU.subtract)

        def weave(z):
            nc.vector.tensor_tensor(
                woven[z][:].rearrange("p (c i) t -> p c t i", i=4),
                gaps[z][:].rearrange("p t (c i) -> p c t i", i=4),
                factor[z][:].unsqueeze(1).unsqueeze(3).broadcast_to([P, J // 4, PACK, 4]),
                ALU.mult,
            )

        def quantise(z, j0, j1):
            nc.vector.quantize_mx(
                out=u_codes[z][:, j0:j1].bitcast(E5X4),
                scales=u_scales[z][:, j0:j1],
                in_=woven[z][:, j0:j1, :].rearrange("p j t -> p (j t)"),
            )

        def gather_words(z):
            nc.vector.tensor_copy(k_codes[z][:], words[z][:].bitcast(U32).indirect(list3[:]))

        def gather_scales(z):
            nc.vector.tensor_copy(k_scales[z][:], scales[:, z, :].indirect(list3[:]))

        def multiply(z):
            for m in range(J // P):
                rows = slice(m * P, (m + 1) * P)
                nc.tensor.matmul_mx(
                    out=acc[m][:],
                    lhsT=u_codes[z][:, rows].bitcast(E5X4),
                    lhsT_scale=u_scales[z][:, rows],
                    rhs=k_codes[z][:].bitcast(E5X4),
                    rhs_scale=k_scales[z][:],
                    start=(z == 0),
                    stop=(z == PASSES - 1),
                )

        for m in range(2):
            nc.tensor.transpose(bias_ps[:, m, :], bias_col[:, m : m + 1].to_broadcast([P, P]), ident[:])

        for q0, q1 in GROUPS:
            gap_planes(q0, q1)
            if q1 == PACK:
                weave(0)
                gather_scales(0)
                quantise(0, 0, J)
                gather_scales(1)
        gather_words(0)
        weave(1)
        multiply(0)
        gather_words(1)
        for m in range(J // P):
            quantise(1, m * P, (m + 1) * P)
        multiply(1)
        nc.scalar.copy(bias[:].rearrange("p (r m) -> p r m", m=2), bias_ps[:].rearrange("p m r -> p r m"))

        steps = [keep.tile([P, I], F32, name="steps%d" % m) for m in range(J // P)]
        result = [keep.tile([P, I], F32, name="result%d" % m) for m in range(J // P)]
        for m in range(J // P):
            nc.vector.tensor_tensor(scores[m][:, PAD:], acc[m][:], bias[:], ALU.add)
        for m in range(J // P):
            nc.vector.tensor_tensor(steps[m][:], scores[m][:, PAD:], scores[m][:, PAD - 1 : PAD - 1 + I], ALU.subtract)
            nc.scalar.activation(result[m][:], steps[m][:], ACT.Abs)
            (nc.sync if m == 0 else nc.scalar).dma_start(out=out[m * P : (m + 1) * P, :], in_=result[m][:])
